import numpy as np
import ml_dtypes


def mxq(x, axis, fmt="e4m3"):
    dtype, down = {"e4m3": (ml_dtypes.float8_e4m3fn, 7), "e5m2": (ml_dtypes.float8_e5m2, 14)}[fmt]
    v = np.moveaxis(np.asarray(x, np.float32).astype(ml_dtypes.bfloat16).astype(np.float64), axis, -1)
    blocks = v.reshape(v.shape[:-1] + (-1, 32))
    amax = np.abs(blocks).max(-1, keepdims=True)
    byte = np.maximum(np.where(amax > 0, np.frexp(amax)[1] - 1 + 127, 0) - down, 1)
    scale = np.exp2(byte - 127.0)
    codes = (blocks / scale).astype(np.float32).astype(dtype).astype(np.float64)
    return np.moveaxis((codes * scale).reshape(v.shape), -1, axis)


WIDE = False


def mx_kscale(k):
    if not WIDE:
        return np.ones(k)
    levels = np.array([10, -10, 5, -5, 0])
    if k % 512:
        return np.exp2(np.random.permutation(np.resize(levels, k // 32))).repeat(32)
    a = np.empty((k // 512, 16))
    for p in range(k // 512):
        a[p, :8] = np.random.permutation(np.resize(levels, 8))
        for g in range(8):
            far = levels[np.abs(levels - a[p, g]) >= 10]
            a[p, g + 8] = far[np.random.randint(len(far))]
    return np.exp2(a.ravel()).repeat(32)


def f64(x):
    return np.asarray(x).astype(np.float64)


def striped(idx):
    return np.tile(idx.reshape(-1, 16).T, (8, 1)).astype(np.uint16)


def unstriped(offs):
    return offs[:16].T.reshape(-1).astype(np.int64)


def pack_weight(w):
    k, n = w.shape
    w = f64(np.asarray(w, np.float32).astype(ml_dtypes.bfloat16)).reshape(k // 32, 32, n)
    amax = np.abs(w).max(1)
    byte = np.clip(np.where(amax > 0, np.frexp(amax)[1] - 1 + 127 - 7, 1), 1, 254)
    scaled = (w * np.exp2(127.0 - byte)[:, None, :]).reshape(k, n).astype(np.float32)
    words = np.ascontiguousarray(scaled.reshape(k // 512, 128, 4, n).transpose(0, 1, 3, 2)).astype(ml_dtypes.float8_e4m3fn).view(np.uint8)
    return words, np.ascontiguousarray(byte.astype(np.uint8).reshape(k // 512, 16, n))


def unpack_weight(words, scales):
    g, p, n, _ = words.shape
    vals = np.ascontiguousarray(words).view(ml_dtypes.float8_e4m3fn).astype(np.float64) * np.repeat(np.exp2(scales.astype(np.float64) - 127.0), 8, axis=1)[..., None]
    return vals.transpose(0, 1, 3, 2).reshape(g * 512, n)


E2M1 = np.array([0.0, 0.5, 1.0, 1.5, 2.0, 3.0, 4.0, 6.0, -0.0, -0.5, -1.0, -1.5, -2.0, -3.0, -4.0, -6.0])


def pack_fp4(w):
    k, n = w.shape
    w = f64(np.asarray(w, np.float32).astype(ml_dtypes.bfloat16)).reshape(k // 32, 32, n)
    amax = np.abs(w).max(1)
    mant, ex = np.frexp(amax / 6.0)
    byte = np.clip(np.where(amax > 0, np.where(mant > 0.5, ex, ex - 1) + 127, 1), 1, 254)
    scaled = (w * np.exp2(127.0 - byte)[:, None, :]).reshape(k, n).astype(np.float32)
    c = np.ascontiguousarray(scaled.reshape(k // 512, 128, 4, n).transpose(0, 1, 3, 2)).astype(ml_dtypes.float4_e2m1fn).view(np.uint8) & 0xF
    words = (c[..., 0::2] | (c[..., 1::2] << 4)).reshape(k // 512, 128, 2 * n)
    return np.ascontiguousarray(words), np.ascontiguousarray(byte.astype(np.uint8).reshape(k // 512, 16, n))


def unpack_fp4(words, scales):
    g, _, n = scales.shape
    words = np.ascontiguousarray(words).reshape(g, 128, n, 2)
    nib = np.empty((g, 128, n, 4), np.uint8)
    nib[..., 0::2] = words & 0xF
    nib[..., 1::2] = words >> 4
    vals = E2M1[nib] * np.repeat(np.exp2(scales.astype(np.float64) - 127.0), 8, axis=1)[..., None]
    return vals.transpose(0, 1, 3, 2).reshape(g * 512, n)


def planes(y):
    n, m = y.shape
    v = y.astype(np.float32).astype(ml_dtypes.bfloat16).astype(np.float64).reshape(n // 32, 32, m)
    top = np.abs(v).max(1)
    byte = np.clip(np.where(top > 0, np.frexp(top)[1] - 1 + 127 - 7, 1), 1, 254)
    codes = (v * np.exp2(127.0 - byte)[:, None, :]).reshape(n, m).astype(np.float32).astype(ml_dtypes.float8_e4m3fn).view(np.uint8)
    words = codes.reshape(n // 512, 128, 4, m).transpose(0, 1, 3, 2)
    return np.ascontiguousarray(words), np.ascontiguousarray(byte.astype(np.uint8).reshape(n // 512, 16, m))


K, T, S, N, H = 512, 1024, 512, 512, 512


def setup_inputs():
    n = np.random.standard_normal
    s = mx_kscale(K)[:, None]
    u = mx_kscale(H)
    packed_xT = pack_weight(n((K, T)) * s)
    packed_w1 = pack_fp4(n((K, N)) / np.sqrt(K) / s)
    packed_w2 = pack_fp4(n((K, N)) / np.sqrt(K) / s)
    packed_w3 = pack_fp4(n((H, N)) / np.sqrt(H) / u[:, None])
    return {
        "x_words": packed_xT[0],
        "x_scales": packed_xT[1],
        "w1_words": packed_w1[0],
        "w1_scales": packed_w1[1],
        "w2_words": packed_w2[0],
        "w2_scales": packed_w2[1],
        "unit": (np.random.uniform(0.6, 1.4, (H, 1)) * u[:, None]).astype(np.float32),
        "w3_words": packed_w3[0],
        "w3_scales": packed_w3[1],
        "offs": striped(np.random.permutation(T)[:S]),
        "u1": striped(np.random.permutation(S)),
        "u2": striped(np.random.permutation(S)),
    }


def reference(x_words, x_scales, w1_words, w1_scales, w2_words, w2_scales, unit, w3_words, w3_scales, offs, u1, u2):
    xq = unpack_weight(x_words, x_scales)[:, unstriped(offs)]
    y = unpack_fp4(w1_words, w1_scales).T @ xq
    d0 = np.log(np.exp(y) + 1.0)
    da = d0[:, unstriped(u1)]
    yw = unpack_fp4(w2_words, w2_scales).T @ xq
    wgt = np.log(np.exp(yw) + 1.0)
    d1 = np.minimum(d0, da + 0.4 * wgt)
    db = d1[:, unstriped(u2)]
    cu = wgt[:, unstriped(u1)]
    d2 = np.minimum(d1, db + 0.4 * cu)
    impr = d0 - d2
    dd = d2[:, unstriped(u2)]
    hid = f64(unit) * (impr * wgt + dd)
    out_0 = unpack_fp4(w3_words, w3_scales).T @ mxq(hid, 0, "e4m3")
    return (out_0,) + planes(out_0)

@@ -1,0 +1,204 @@
+from contextlib import ExitStack
+
+import concourse.mybir as mybir
+
+F32 = mybir.dt.float32
+BF16 = mybir.dt.bfloat16
+I32 = mybir.dt.int32
+U32 = mybir.dt.uint32
+U16 = mybir.dt.uint16
+U8 = mybir.dt.uint8
+FP8X4 = mybir.dt.float8_e4m3fn_x4
+FP4X4 = mybir.dt.float4_e2m1fn_x4
+ALU = mybir.AluOpType
+ACT = mybir.ActivationFunctionType
+
+P = 128
+PACK = 4
+T = 1024
+S = 512
+N = 512
+CHUNK = 128
+CHUNKS = S // CHUNK
+TINY = 2.0 ** -60
+STEP = 0.4
+FUSED = (0, 1)
+
+FLOPS = 3 * 2 * 512 * 512 * 512
+
+
+def tile_picked_ybellmf_gain_po_kernel(
+    tc, x_words, x_scales, w1_words, w1_scales, w2_words, w2_scales, unit, w3_words, w3_scales,
+    offs, u1, u2, out_0, out_1, out_2,
+):
+    nc = tc.nc
+    with ExitStack() as ctx:
+        keep = ctx.enter_context(tc.tile_pool(name="keep", bufs=1))
+        psum = ctx.enter_context(tc.psum_pool(name="psum", bufs=1))
+
+        def load_list(src, name):
+            tile = keep.tile([P, S // 16], U16, name=name)
+            nc.sync.dma_start(tile[:], src)
+            return tile
+
+        def load_words(src, dtype, width, name):
+            tile = keep.tile([P, width], dtype, name=name, align_bytes=64)
+            nc.sync.dma_start(tile[:].bitcast(I32), src.bitcast(I32))
+            return tile
+
+        def load_scales(src, width, name):
+            tile = keep.tile([P, width], U8, name=name, align_bytes=64)
+            for q in range(4):
+                rows = src[0, 4 * q : 4 * q + 4, :].bitcast(I32)
+                nc.sync.dma_start(tile[32 * q : 32 * q + 32, :].bitcast(I32), rows.partition_broadcast(8))
+            return tile
+
+        offs_sb = load_list(offs, "offs_sb")
+        xs_all = load_scales(x_scales, T, "xs_all")
+        xw_all = load_words(x_words[0].rearrange("p n t -> p (n t)"), U32, T, "xw_all")
+        w1_raw = load_words(w1_words[0], U8, 2 * N, "w1_raw")
+        s1_raw = load_scales(w1_scales, N, "s1_raw")
+        w2_raw = load_words(w2_words[0], U8, 2 * N, "w2_raw")
+        s2_raw = load_scales(w2_scales, N, "s2_raw")
+        u1_sb = load_list(u1, "u1_sb")
+        u2_sb = load_list(u2, "u2_sb")
+        unit_sb = keep.tile([P, PACK], F32, name="unit_sb")
+        nc.sync.dma_start(unit_sb[:], unit.rearrange("(p t) o -> p (t o)", t=PACK))
+        w3_raw = load_words(w3_words[0], U8, 2 * N, "w3_raw")
+        s3_raw = load_scales(w3_scales, N, "s3_raw")
+
+        tiny = keep.tile([P, 1], F32, name="tiny")
+        nc.gpsimd.memset(tiny[:], TINY)
+
+        def deal_words(raw, name):
+            dealt = keep.tile([P, PACK, 2 * P], U8, name=name, align_bytes=64)
+            nc.vector.tensor_copy(
+                dealt[:].rearrange("p t (m b) -> p t m b", b=2),
+                raw[:].rearrange("p (m t b) -> p t m b", t=PACK, b=2),
+            )
+            return dealt
+
+        def deal_scales(raw, name):
+            dealt = keep.tile([P, PACK, P], U8, name=name, align_bytes=64)
+            nc.vector.tensor_copy(dealt[:], raw[:].rearrange("p (m t) -> p t m", t=PACK))
+            return dealt
+
+        xs = keep.tile([P, S], U8, name="xs", align_bytes=64)
+        nc.vector.tensor_copy(xs[:], xs_all[:].indirect(offs_sb[:]))
+        w1 = deal_words(w1_raw, "w1")
+        xw = keep.tile([P, S], U32, name="xw", align_bytes=64)
+        nc.vector.tensor_copy(xw[:], xw_all[:].indirect(offs_sb[:]))
+        s1 = deal_scales(s1_raw, "s1")
+        w2 = deal_words(w2_raw, "w2")
+        s2 = deal_scales(s2_raw, "s2")
+        w3 = deal_words(w3_raw, "w3")
+        s3 = deal_scales(s3_raw, "s3")
+
+        def product(out, w, s, t, codes, scales):
+            nc.tensor.matmul_mx(
+                out, lhsT=w[:, t, :].bitcast(FP4X4), lhsT_scale=s[:, t, :],
+                rhs=codes.bitcast(FP8X4), rhs_scale=scales, start=True, stop=True,
+            )
+
+        rows = range(PACK)
+        y = [psum.tile([P, S], F32, name=f"y{t}", tag=f"bank{t}") for t in rows]
+        yw = [psum.tile([P, S], F32, name=f"yw{t}", tag=f"bank{PACK + t}") for t in rows]
+        d0_win = [keep.tile([P, 3 * S], F32, name=f"d0_win{t}") for t in rows]
+        wgt_win = [keep.tile([P, 3 * S], F32, name=f"wgt_win{t}") for t in rows]
+        d1_win = [keep.tile([P, 2 * S], F32, name=f"d1_win{t}") for t in rows]
+        d2_win = [keep.tile([P, 2 * S], F32, name=f"d2_win{t}") for t in rows]
+        da = [keep.tile([P, S], F32, name=f"da{t}") for t in rows]
+        cu = [keep.tile([P, S], F32, name=f"cu{t}") for t in rows]
+        gain = [keep.tile([P, S], F32, name=f"gain{t}") for t in rows]
+        dd = [keep.tile([P, S], F32, name=f"dd{t}") for t in rows]
+        hid = keep.tile([P, PACK, S], F32, name="hid")
+        first, second, third = slice(0, S), slice(S, 2 * S), slice(2 * S, 3 * S)
+
+        for t in rows:
+            product(y[t][:], w1, s1, t, xw[:], xs[:])
+            nc.scalar.activation(wgt_win[t][:, second], y[t][:], ACT.Sigmoid, scale=-1.0)
+        for t in rows:
+            product(yw[t][:], w2, s2, t, xw[:], xs[:])
+            nc.scalar.activation(wgt_win[t][:, third], yw[t][:], ACT.Sigmoid, scale=-1.0)
+
+        def softplus(t):
+            nc.scalar.activation(d0_win[t][:, S:], wgt_win[t][:, S:], ACT.Ln, bias=tiny[:])
+            nc.vector.scalar_tensor_tensor(d0_win[t][:, first], d0_win[t][:, second], -1.0, y[t][:], ALU.mult, ALU.max)
+            nc.vector.scalar_tensor_tensor(wgt_win[t][:, first], d0_win[t][:, third], -1.0, yw[t][:], ALU.mult, ALU.max)
+
+        def round_one(t):
+            nc.scalar.activation(da[t][:], d0_win[t][:].indirect(u1_sb[:]), ACT.Copy)
+            nc.scalar.activation(cu[t][:], wgt_win[t][:].indirect(u1_sb[:]), ACT.Copy, scale=STEP)
+            nc.vector.scalar_tensor_tensor(d1_win[t][:, second], wgt_win[t][:, first], STEP, da[t][:], ALU.mult, ALU.add)
+            nc.vector.tensor_tensor(d1_win[t][:, first], d0_win[t][:, first], d1_win[t][:, second], ALU.min)
+
+        def round_two(t):
+            if t in FUSED:
+                nc.vector.tensor_tensor(d2_win[t][:, second], d1_win[t][:].indirect(u2_sb[:]), cu[t][:], ALU.add)
+            else:
+                db = keep.tile([P, S], F32, name=f"db{t}")
+                nc.scalar.activation(db[:], d1_win[t][:].indirect(u2_sb[:]), ACT.Copy)
+                nc.vector.tensor_tensor(d2_win[t][:, second], db[:], cu[t][:], ALU.add)
+            nc.vector.tensor_tensor(d2_win[t][:, first], d1_win[t][:, first], d2_win[t][:, second], ALU.min)
+
+        def hidden(t, c0, c1):
+            cols = slice(c0, c1)
+            nc.scalar.activation(dd[t][:, cols], d2_win[t][:].indirect(u2_sb[:, c0 // 16 : c1 // 16]), ACT.Copy)
+            nc.vector.tensor_tensor(da[t][:, cols], d0_win[t][:, cols], d2_win[t][:, cols], ALU.subtract)
+            nc.vector.scalar_tensor_tensor(gain[t][:, cols], da[t][:, cols], unit_sb[:, t : t + 1], wgt_win[t][:, cols], ALU.mult, ALU.mult)
+            nc.vector.scalar_tensor_tensor(hid[:, t, cols], dd[t][:, cols], unit_sb[:, t : t + 1], gain[t][:, cols], ALU.mult, ALU.add)
+
+        softplus(0)
+        softplus(1)
+        round_one(0)
+        round_one(1)
+        softplus(2)
+        round_two(0)
+        softplus(3)
+        round_two(1)
+        round_one(2)
+        round_one(3)
+        hidden(0, 0, S)
+        round_two(2)
+        hidden(1, 0, S)
+        round_two(3)
+        hidden(2, 0, S)
+
+        out_codes = keep.tile([P, S], U32, name="out_codes", align_bytes=64)
+        out_scales = keep.tile([P, S], U8, name="out_scales", align_bytes=64)
+        out_rows = out_0.rearrange("(p t) j -> p t j", t=PACK)
+        out_words = out_1[0].rearrange("p n t -> p (n t)").bitcast(I32)
+
+        def last_product(c):
+            cols = slice(c * CHUNK, (c + 1) * CHUNK)
+            hidden(PACK - 1, c * CHUNK, (c + 1) * CHUNK)
+            woven = keep.tile([P, CHUNK, PACK], BF16, name=f"woven{c}", align_bytes=64)
+            nc.vector.tensor_copy(
+                woven[:].rearrange("p (g i) t -> p g t i", i=4),
+                hid[:, :, cols].rearrange("p t (g i) -> p g t i", i=4),
+            )
+            codes = keep.tile([P, CHUNK], U32, name=f"codes{c}", align_bytes=64)
+            scales = keep.tile([P, CHUNK], U8, name=f"scales{c}", align_bytes=64)
+            nc.vector.quantize_mx(codes[:].bitcast(FP8X4), scales[:], woven[:].rearrange("p j t -> p (j t)"))
+            acc = psum.tile([P, PACK, CHUNK], F32, name=f"acc{c}", tag=f"bank{c}")
+            for t in rows:
+                product(acc[:, t, :], w3, s3, t, codes[:], scales[:])
+            return acc
+
+        def hand_out(c, acc):
+            cols = slice(c * CHUNK, (c + 1) * CHUNK)
+            rounded = keep.tile([P, CHUNK, PACK], BF16, name=f"rounded{c}", align_bytes=64)
+            nc.scalar.copy(rounded[:], acc[:].rearrange("p t j -> p j t"))
+            result = keep.tile([P, PACK, CHUNK], F32, name=f"result{c}")
+            nc.scalar.copy(result[:], acc[:])
+            nc.sync.dma_start(out_rows[:, :, cols], result[:])
+            nc.vector.quantize_mx(out_codes[:, cols].bitcast(FP8X4), out_scales[:, cols], rounded[:].rearrange("p j t -> p (j t)"))
+            nc.sync.dma_start(out_words[:, cols], out_codes[:, cols].bitcast(I32))
+
+        accs = [last_product(0)]
+        for c in range(1, CHUNKS):
+            accs.append(last_product(c))
+            hand_out(c - 1, accs[c - 1])
+        hand_out(CHUNKS - 1, accs[CHUNKS - 1])
+        for q in range(4):
+            nc.sync.dma_start(out_2[0, 4 * q : 4 * q + 4, :].bitcast(I32), out_scales[32 * q : 32 * q + 4, :].bitcast(I32))

@@ -22,7 +22,9 @@ CHUNK = 128
 CHUNKS = S // CHUNK
 TINY = 2.0 ** -60
 STEP = 0.4
-FUSED = (0, 1)
+HALF = S // 2
+FUSED = (0,)
+SKEW = 2
 
 FLOPS = 3 * 2 * 512 * 512 * 512
 
@@ -41,31 +43,34 @@ def tile_picked_ybellmf_gain_po_kernel(
             nc.sync.dma_start(tile[:], src)
             return tile
 
-        def load_words(src, dtype, width, name):
-            tile = keep.tile([P, width], dtype, name=name, align_bytes=64)
+        def load_words(tile, src):
             nc.sync.dma_start(tile[:].bitcast(I32), src.bitcast(I32))
-            return tile
 
-        def load_scales(src, width, name):
-            tile = keep.tile([P, width], U8, name=name, align_bytes=64)
+        def load_scales(tile, src):
             for q in range(4):
-                rows = src[0, 4 * q : 4 * q + 4, :].bitcast(I32)
-                nc.sync.dma_start(tile[32 * q : 32 * q + 32, :].bitcast(I32), rows.partition_broadcast(8))
-            return tile
+                nc.sync.dma_start(tile[32 * q : 32 * q + 4, :].bitcast(I32), src[0, 4 * q : 4 * q + 4, :].bitcast(I32))
+
+        xs_all = keep.tile([P, T], U8, name="xs_all", align_bytes=64)
+        xw_all = keep.tile([P, T], U32, name="xw_all", align_bytes=64)
+        w1_raw = keep.tile([P, 2 * N], U8, name="w1_raw", align_bytes=64)
+        s1_raw = keep.tile([P, N], U8, name="s1_raw", tag="s1_raw_then_xw", align_bytes=64)
+        w23_raw = keep.tile([P, 2 * N], U8, name="w23_raw", align_bytes=64)
+        s23_raw = keep.tile([P, N], U8, name="s23_raw", align_bytes=64)
+        nc.gpsimd.memset(xs_all[:].bitcast(I32), 0)
+        nc.gpsimd.memset(s1_raw[:].bitcast(I32), 0)
+        nc.gpsimd.memset(s23_raw[:].bitcast(I32), 0)
 
         offs_sb = load_list(offs, "offs_sb")
-        xs_all = load_scales(x_scales, T, "xs_all")
-        xw_all = load_words(x_words[0].rearrange("p n t -> p (n t)"), U32, T, "xw_all")
-        w1_raw = load_words(w1_words[0], U8, 2 * N, "w1_raw")
-        s1_raw = load_scales(w1_scales, N, "s1_raw")
-        w2_raw = load_words(w2_words[0], U8, 2 * N, "w2_raw")
-        s2_raw = load_scales(w2_scales, N, "s2_raw")
+        load_words(w1_raw, w1_words[0])
+        load_scales(xs_all, x_scales)
+        load_words(xw_all, x_words[0].rearrange("p n t -> p (n t)"))
+        load_scales(s1_raw, w1_scales)
+        load_words(w23_raw, w2_words[0])
+        load_scales(s23_raw, w2_scales)
         u1_sb = load_list(u1, "u1_sb")
         u2_sb = load_list(u2, "u2_sb")
         unit_sb = keep.tile([P, PACK], F32, name="unit_sb")
         nc.sync.dma_start(unit_sb[:], unit.rearrange("(p t) o -> p (t o)", t=PACK))
-        w3_raw = load_words(w3_words[0], U8, 2 * N, "w3_raw")
-        s3_raw = load_scales(w3_scales, N, "s3_raw")
 
         tiny = keep.tile([P, 1], F32, name="tiny")
         nc.gpsimd.memset(tiny[:], TINY)
@@ -78,21 +83,29 @@ def tile_picked_ybellmf_gain_po_kernel(
             )
             return dealt
 
-        def deal_scales(raw, name):
+        def deal_scales(raw, name, pieces=(slice(0, PACK),)):
             dealt = keep.tile([P, PACK, P], U8, name=name, align_bytes=64)
-            nc.vector.tensor_copy(dealt[:], raw[:].rearrange("p (m t) -> p t m", t=PACK))
+            for ts in pieces:
+                nc.vector.tensor_copy(dealt[:, ts, :], raw[:].rearrange("p (m t) -> p t m", t=PACK)[:, ts, :])
             return dealt
 
-        xs = keep.tile([P, S], U8, name="xs", align_bytes=64)
-        nc.vector.tensor_copy(xs[:], xs_all[:].indirect(offs_sb[:]))
+        def gather_half(table, dtype, h, name, tag):
+            tile = keep.tile([P, HALF], dtype, name=name, tag=tag, align_bytes=64)
+            nc.vector.tensor_copy(tile[:], table[:].indirect(offs_sb[:, h * HALF // 16 : (h + 1) * HALF // 16]))
+            return tile
+
         w1 = deal_words(w1_raw, "w1")
-        xw = keep.tile([P, S], U32, name="xw", align_bytes=64)
-        nc.vector.tensor_copy(xw[:], xw_all[:].indirect(offs_sb[:]))
-        s1 = deal_scales(s1_raw, "s1")
-        w2 = deal_words(w2_raw, "w2")
-        s2 = deal_scales(s2_raw, "s2")
-        w3 = deal_words(w3_raw, "w3")
-        s3 = deal_scales(s3_raw, "s3")
+        xs = [gather_half(xs_all, U8, 0, "xs0", "xs0")]
+        xw = [gather_half(xw_all, U32, 0, "xw0", "xw0")]
+        s1 = deal_scales(s1_raw, "s1", (slice(0, 1), slice(1, PACK)))
+        xs.append(gather_half(xs_all, U8, 1, "xs1", "xs1"))
+        xw.append(gather_half(xw_all, U32, 1, "xw1", "s1_raw_then_xw"))
+        w2 = deal_words(w23_raw, "w2")
+        s2 = deal_scales(s23_raw, "s2")
+        load_words(w23_raw, w3_words[0])
+        load_scales(s23_raw, w3_scales)
+        w3 = deal_words(w23_raw, "w3")
+        s3 = deal_scales(s23_raw, "s3")
 
         def product(out, w, s, t, codes, scales):
             nc.tensor.matmul_mx(
@@ -109,60 +122,87 @@ def tile_picked_ybellmf_gain_po_kernel(
         d2_win = [keep.tile([P, 2 * S], F32, name=f"d2_win{t}") for t in rows]
         da = [keep.tile([P, S], F32, name=f"da{t}") for t in rows]
         cu = [keep.tile([P, S], F32, name=f"cu{t}") for t in rows]
-        gain = [keep.tile([P, S], F32, name=f"gain{t}") for t in rows]
-        dd = [keep.tile([P, S], F32, name=f"dd{t}") for t in rows]
+        db = [keep.tile([P, S], F32, name=f"db{t}") for t in rows]
+        gain = keep.tile([P, PACK, S], F32, name="gain")
+        dd = keep.tile([P, PACK, S], F32, name="dd")
         hid = keep.tile([P, PACK, S], F32, name="hid")
         first, second, third = slice(0, S), slice(S, 2 * S), slice(2 * S, 3 * S)
 
+        for h in range(2):
+            for t in rows:
+                cols = slice(h * HALF, (h + 1) * HALF)
+                product(y[t][:, cols], w1, s1, t, xw[h][:], xs[h][:])
+                nc.scalar.activation(wgt_win[t][:, S + h * HALF : S + (h + 1) * HALF], y[t][:, cols], ACT.Sigmoid, scale=-1.0)
         for t in rows:
-            product(y[t][:], w1, s1, t, xw[:], xs[:])
-            nc.scalar.activation(wgt_win[t][:, second], y[t][:], ACT.Sigmoid, scale=-1.0)
-        for t in rows:
-            product(yw[t][:], w2, s2, t, xw[:], xs[:])
+            for h in range(2):
+                product(yw[t][:, h * HALF : (h + 1) * HALF], w2, s2, t, xw[h][:], xs[h][:])
             nc.scalar.activation(wgt_win[t][:, third], yw[t][:], ACT.Sigmoid, scale=-1.0)
 
-        def softplus(t):
-            nc.scalar.activation(d0_win[t][:, S:], wgt_win[t][:, S:], ACT.Ln, bias=tiny[:])
-            nc.vector.scalar_tensor_tensor(d0_win[t][:, first], d0_win[t][:, second], -1.0, y[t][:], ALU.mult, ALU.max)
-            nc.vector.scalar_tensor_tensor(wgt_win[t][:, first], d0_win[t][:, third], -1.0, yw[t][:], ALU.mult, ALU.max)
+        def logarithms(t):
+            if t in FUSED:
+                nc.scalar.activation(d0_win[t][:, third], wgt_win[t][:, third], ACT.Ln, bias=tiny[:])
+                nc.scalar.activation(d0_win[t][:, second], wgt_win[t][:, second], ACT.Ln, bias=tiny[:])
+            else:
+                nc.scalar.activation(d0_win[t][:, S:], wgt_win[t][:, S:], ACT.Ln, bias=tiny[:])
 
-        def round_one(t):
-            nc.scalar.activation(da[t][:], d0_win[t][:].indirect(u1_sb[:]), ACT.Copy)
+        def softplus(t):
+            if t in FUSED:
+                nc.vector.scalar_tensor_tensor(wgt_win[t][:, first], d0_win[t][:, third], -1.0, yw[t][:], ALU.mult, ALU.max)
+                nc.vector.tensor_scalar(da[t][:], wgt_win[t][:, first], STEP, None, ALU.mult)
+                nc.vector.scalar_tensor_tensor(d0_win[t][:, first], d0_win[t][:, second], -1.0, y[t][:], ALU.mult, ALU.max)
+            else:
+                nc.vector.scalar_tensor_tensor(d0_win[t][:, first], d0_win[t][:, second], -1.0, y[t][:], ALU.mult, ALU.max)
+                nc.vector.scalar_tensor_tensor(wgt_win[t][:, first], d0_win[t][:, third], -1.0, yw[t][:], ALU.mult, ALU.max)
+
+        def fetch_da(t):
+            if t not in FUSED:
+                nc.scalar.activation(da[t][:], d0_win[t][:].indirect(u1_sb[:]), ACT.Copy)
+
+        def fetch_cu(t):
             nc.scalar.activation(cu[t][:], wgt_win[t][:].indirect(u1_sb[:]), ACT.Copy, scale=STEP)
-            nc.vector.scalar_tensor_tensor(d1_win[t][:, second], wgt_win[t][:, first], STEP, da[t][:], ALU.mult, ALU.add)
+
+        def offer_one(t):
+            if t in FUSED:
+                nc.vector.tensor_tensor(d1_win[t][:, second], d0_win[t][:].indirect(u1_sb[:]), da[t][:], ALU.add)
+            else:
+                nc.vector.scalar_tensor_tensor(d1_win[t][:, second], wgt_win[t][:, first], STEP, da[t][:], ALU.mult, ALU.add)
+
+        def relax_one(t):
             nc.vector.tensor_tensor(d1_win[t][:, first], d0_win[t][:, first], d1_win[t][:, second], ALU.min)
 
-        def round_two(t):
+        def fetch_db(t):
+            if t not in FUSED:
+                nc.scalar.activation(db[t][:], d1_win[t][:].indirect(u2_sb[:]), ACT.Copy)
+
+        def offer_two(t):
             if t in FUSED:
                 nc.vector.tensor_tensor(d2_win[t][:, second], d1_win[t][:].indirect(u2_sb[:]), cu[t][:], ALU.add)
             else:
-                db = keep.tile([P, S], F32, name=f"db{t}")
-                nc.scalar.activation(db[:], d1_win[t][:].indirect(u2_sb[:]), ACT.Copy)
-                nc.vector.tensor_tensor(d2_win[t][:, second], db[:], cu[t][:], ALU.add)
+                nc.vector.tensor_tensor(d2_win[t][:, second], db[t][:], cu[t][:], ALU.add)
+
+        def relax_two(t):
             nc.vector.tensor_tensor(d2_win[t][:, first], d1_win[t][:, first], d2_win[t][:, second], ALU.min)
 
-        def hidden(t, c0, c1):
-            cols = slice(c0, c1)
-            nc.scalar.activation(dd[t][:, cols], d2_win[t][:].indirect(u2_sb[:, c0 // 16 : c1 // 16]), ACT.Copy)
+        def improvement(t, cols=first):
             nc.vector.tensor_tensor(da[t][:, cols], d0_win[t][:, cols], d2_win[t][:, cols], ALU.subtract)
-            nc.vector.scalar_tensor_tensor(gain[t][:, cols], da[t][:, cols], unit_sb[:, t : t + 1], wgt_win[t][:, cols], ALU.mult, ALU.mult)
-            nc.vector.scalar_tensor_tensor(hid[:, t, cols], dd[t][:, cols], unit_sb[:, t : t + 1], gain[t][:, cols], ALU.mult, ALU.add)
 
-        softplus(0)
-        softplus(1)
-        round_one(0)
-        round_one(1)
-        softplus(2)
-        round_two(0)
-        softplus(3)
-        round_two(1)
-        round_one(2)
-        round_one(3)
-        hidden(0, 0, S)
-        round_two(2)
-        hidden(1, 0, S)
-        round_two(3)
-        hidden(2, 0, S)
+        def weigh(t, cols=first):
+            nc.vector.scalar_tensor_tensor(gain[:, t, cols], da[t][:, cols], unit_sb[:, t : t + 1], wgt_win[t][:, cols], ALU.mult, ALU.mult)
+
+        def fetch_dd(t, cols=first):
+            picks = u2_sb[:, cols.start // 16 : cols.stop // 16]
+            nc.scalar.activation(dd[:, t, cols], d2_win[t][:].indirect(picks), ACT.Copy)
+
+        def combine(t, cols=first):
+            nc.vector.scalar_tensor_tensor(hid[:, t, cols], dd[:, t, cols], unit_sb[:, t : t + 1], gain[:, t, cols], ALU.mult, ALU.add)
+
+        relax = [logarithms, softplus, fetch_da, offer_one, relax_one, fetch_cu, fetch_db, offer_two, relax_two]
+        whole = relax + [fetch_dd, improvement, weigh, combine]
+        for k in range(len(whole) + SKEW * (PACK - 1)):
+            for t in rows:
+                stages = relax if t == PACK - 1 else whole
+                if 0 <= k - SKEW * t < len(stages):
+                    stages[k - SKEW * t](t)
 
         out_codes = keep.tile([P, S], U32, name="out_codes", align_bytes=64)
         out_scales = keep.tile([P, S], U8, name="out_scales", align_bytes=64)
@@ -171,7 +211,10 @@ def tile_picked_ybellmf_gain_po_kernel(
 
         def last_product(c):
             cols = slice(c * CHUNK, (c + 1) * CHUNK)
-            hidden(PACK - 1, c * CHUNK, (c + 1) * CHUNK)
+            fetch_dd(PACK - 1, cols)
+            improvement(PACK - 1, cols)
+            weigh(PACK - 1, cols)
+            combine(PACK - 1, cols)
             woven = keep.tile([P, CHUNK, PACK], BF16, name=f"woven{c}", align_bytes=64)
             nc.vector.tensor_copy(
                 woven[:].rearrange("p (g i) t -> p g t i", i=4),

@@ -23,8 +23,10 @@ CHUNKS = S // CHUNK
 TINY = 2.0 ** -60
 STEP = 0.4
 HALF = S // 2
-FUSED = (0,)
-SKEW = 2
+FUSED = (0, 1)
+FUSED_TWO = ()
+SKEW = 3
+EARLY = 2
 
 FLOPS = 3 * 2 * 512 * 512 * 512
 
@@ -139,7 +141,7 @@ def tile_picked_ybellmf_gain_po_kernel(
             nc.scalar.activation(wgt_win[t][:, third], yw[t][:], ACT.Sigmoid, scale=-1.0)
 
         def logarithms(t):
-            if t in FUSED:
+            if t == 0:
                 nc.scalar.activation(d0_win[t][:, third], wgt_win[t][:, third], ACT.Ln, bias=tiny[:])
                 nc.scalar.activation(d0_win[t][:, second], wgt_win[t][:, second], ACT.Ln, bias=tiny[:])
             else:
@@ -171,11 +173,11 @@ def tile_picked_ybellmf_gain_po_kernel(
             nc.vector.tensor_tensor(d1_win[t][:, first], d0_win[t][:, first], d1_win[t][:, second], ALU.min)
 
         def fetch_db(t):
-            if t not in FUSED:
+            if t not in FUSED_TWO:
                 nc.scalar.activation(db[t][:], d1_win[t][:].indirect(u2_sb[:]), ACT.Copy)
 
         def offer_two(t):
-            if t in FUSED:
+            if t in FUSED_TWO:
                 nc.vector.tensor_tensor(d2_win[t][:, second], d1_win[t][:].indirect(u2_sb[:]), cu[t][:], ALU.add)
             else:
                 nc.vector.tensor_tensor(d2_win[t][:, second], db[t][:], cu[t][:], ALU.add)
@@ -200,7 +202,7 @@ def tile_picked_ybellmf_gain_po_kernel(
         whole = relax + [fetch_dd, improvement, weigh, combine]
         for k in range(len(whole) + SKEW * (PACK - 1)):
             for t in rows:
-                stages = relax if t == PACK - 1 else whole
+                stages = whole if t < EARLY else relax
                 if 0 <= k - SKEW * t < len(stages):
                     stages[k - SKEW * t](t)
 
@@ -211,12 +213,13 @@ def tile_picked_ybellmf_gain_po_kernel(
 
         def last_product(c):
             cols = slice(c * CHUNK, (c + 1) * CHUNK)
-            fetch_dd(PACK - 1, cols)
-            improvement(PACK - 1, cols)
-            weigh(PACK - 1, cols)
-            combine(PACK - 1, cols)
+            if c * CHUNK % HALF == 0:
+                for stage in whole[len(relax) :]:
+                    for t in range(EARLY, PACK):
+                        stage(t, slice(c * CHUNK, c * CHUNK + HALF))
             woven = keep.tile([P, CHUNK, PACK], BF16, name=f"woven{c}", align_bytes=64)
-            nc.vector.tensor_copy(
+            weave = nc.scalar.copy if c < CHUNKS // 2 else nc.vector.tensor_copy
+            weave(
                 woven[:].rearrange("p (g i) t -> p g t i", i=4),
                 hid[:, :, cols].rearrange("p t (g i) -> p g t i", i=4),
             )
@@ -231,9 +234,16 @@ def tile_picked_ybellmf_gain_po_kernel(
         def hand_out(c, acc):
             cols = slice(c * CHUNK, (c + 1) * CHUNK)
             rounded = keep.tile([P, CHUNK, PACK], BF16, name=f"rounded{c}", align_bytes=64)
-            nc.scalar.copy(rounded[:], acc[:].rearrange("p t j -> p j t"))
             result = keep.tile([P, PACK, CHUNK], F32, name=f"result{c}")
-            nc.scalar.copy(result[:], acc[:])
+            if c < CHUNKS - 1:
+                nc.scalar.copy(result[:], acc[:])
+                nc.scalar.copy(rounded[:], acc[:].rearrange("p t j -> p j t"))
+            else:
+                nc.vector.tensor_copy(result[:], acc[:])
+                nc.vector.tensor_copy(
+                    rounded[:].rearrange("p (g i) t -> p g t i", i=4),
+                    result[:].rearrange("p t (g i) -> p g t i", i=4),
+                )
             nc.sync.dma_start(out_rows[:, :, cols], result[:])
             nc.vector.quantize_mx(out_codes[:, cols].bitcast(FP8X4), out_scales[:, cols], rounded[:].rearrange("p j t -> p (j t)"))
             nc.sync.dma_start(out_words[:, cols], out_codes[:, cols].bitcast(I32))
@@ -244,4 +254,5 @@ def tile_picked_ybellmf_gain_po_kernel(
             hand_out(c - 1, accs[c - 1])
         hand_out(CHUNKS - 1, accs[CHUNKS - 1])
         for q in range(4):
-            nc.sync.dma_start(out_2[0, 4 * q : 4 * q + 4, :].bitcast(I32), out_scales[32 * q : 32 * q + 4, :].bitcast(I32))
+            queue = nc.scalar if q % 2 else nc.sync
+            queue.dma_start(out_2[0, 4 * q : 4 * q + 4, :].bitcast(I32), out_scales[32 * q : 32 * q + 4, :].bitcast(I32))

from contextlib import ExitStack

import concourse.mybir as mybir

F32 = mybir.dt.float32
BF16 = mybir.dt.bfloat16
I32 = mybir.dt.int32
U32 = mybir.dt.uint32
U16 = mybir.dt.uint16
U8 = mybir.dt.uint8
FP8X4 = mybir.dt.float8_e4m3fn_x4
FP4X4 = mybir.dt.float4_e2m1fn_x4
ALU = mybir.AluOpType
ACT = mybir.ActivationFunctionType

P = 128
PACK = 4
T = 1024
S = 512
N = 512
CHUNK = 128
CHUNKS = S // CHUNK
TINY = 2.0 ** -60
STEP = 0.4
HALF = S // 2
FUSED = (0, 1)
FUSED_TWO = ()
SKEW = 3
EARLY = 2

FLOPS = 3 * 2 * 512 * 512 * 512


def tile_picked_ybellmf_gain_po_kernel(
    tc, x_words, x_scales, w1_words, w1_scales, w2_words, w2_scales, unit, w3_words, w3_scales,
    offs, u1, u2, out_0, out_1, out_2,
):
    nc = tc.nc
    with ExitStack() as ctx:
        keep = ctx.enter_context(tc.tile_pool(name="keep", bufs=1))
        psum = ctx.enter_context(tc.psum_pool(name="psum", bufs=1))

        def load_list(src, name):
            tile = keep.tile([P, S // 16], U16, name=name)
            nc.sync.dma_start(tile[:], src)
            return tile

        def load_words(tile, src):
            nc.sync.dma_start(tile[:].bitcast(I32), src.bitcast(I32))

        def load_scales(tile, src):
            for q in range(4):
                nc.sync.dma_start(tile[32 * q : 32 * q + 4, :].bitcast(I32), src[0, 4 * q : 4 * q + 4, :].bitcast(I32))

        xs_all = keep.tile([P, T], U8, name="xs_all", align_bytes=64)
        xw_all = keep.tile([P, T], U32, name="xw_all", align_bytes=64)
        w1_raw = keep.tile([P, 2 * N], U8, name="w1_raw", align_bytes=64)
        s1_raw = keep.tile([P, N], U8, name="s1_raw", tag="s1_raw_then_xw", align_bytes=64)
        w23_raw = keep.tile([P, 2 * N], U8, name="w23_raw", align_bytes=64)
        s23_raw = keep.tile([P, N], U8, name="s23_raw", align_bytes=64)
        nc.gpsimd.memset(xs_all[:].bitcast(I32), 0)
        nc.gpsimd.memset(s1_raw[:].bitcast(I32), 0)
        nc.gpsimd.memset(s23_raw[:].bitcast(I32), 0)

        offs_sb = load_list(offs, "offs_sb")
        load_words(w1_raw, w1_words[0])
        load_scales(xs_all, x_scales)
        load_words(xw_all, x_words[0].rearrange("p n t -> p (n t)"))
        load_scales(s1_raw, w1_scales)
        load_words(w23_raw, w2_words[0])
        load_scales(s23_raw, w2_scales)
        u1_sb = load_list(u1, "u1_sb")
        u2_sb = load_list(u2, "u2_sb")
        unit_sb = keep.tile([P, PACK], F32, name="unit_sb")
        nc.sync.dma_start(unit_sb[:], unit.rearrange("(p t) o -> p (t o)", t=PACK))

        tiny = keep.tile([P, 1], F32, name="tiny")
        nc.gpsimd.memset(tiny[:], TINY)

        def deal_words(raw, name):
            dealt = keep.tile([P, PACK, 2 * P], U8, name=name, align_bytes=64)
            nc.vector.tensor_copy(
                dealt[:].rearrange("p t (m b) -> p t m b", b=2),
                raw[:].rearrange("p (m t b) -> p t m b", t=PACK, b=2),
            )
            return dealt

        def deal_scales(raw, name, pieces=(slice(0, PACK),)):
            dealt = keep.tile([P, PACK, P], U8, name=name, align_bytes=64)
            for ts in pieces:
                nc.vector.tensor_copy(dealt[:, ts, :], raw[:].rearrange("p (m t) -> p t m", t=PACK)[:, ts, :])
            return dealt

        def gather_half(table, dtype, h, name, tag):
            tile = keep.tile([P, HALF], dtype, name=name, tag=tag, align_bytes=64)
            nc.vector.tensor_copy(tile[:], table[:].indirect(offs_sb[:, h * HALF // 16 : (h + 1) * HALF // 16]))
            return tile

        w1 = deal_words(w1_raw, "w1")
        xs = [gather_half(xs_all, U8, 0, "xs0", "xs0")]
        xw = [gather_half(xw_all, U32, 0, "xw0", "xw0")]
        s1 = deal_scales(s1_raw, "s1", (slice(0, 1), slice(1, PACK)))
        xs.append(gather_half(xs_all, U8, 1, "xs1", "xs1"))
        xw.append(gather_half(xw_all, U32, 1, "xw1", "s1_raw_then_xw"))
        w2 = deal_words(w23_raw, "w2")
        s2 = deal_scales(s23_raw, "s2")
        load_words(w23_raw, w3_words[0])
        load_scales(s23_raw, w3_scales)
        w3 = deal_words(w23_raw, "w3")
        s3 = deal_scales(s23_raw, "s3")

        def product(out, w, s, t, codes, scales):
            nc.tensor.matmul_mx(
                out, lhsT=w[:, t, :].bitcast(FP4X4), lhsT_scale=s[:, t, :],
                rhs=codes.bitcast(FP8X4), rhs_scale=scales, start=True, stop=True,
            )

        rows = range(PACK)
        y = [psum.tile([P, S], F32, name=f"y{t}", tag=f"bank{t}") for t in rows]
        yw = [psum.tile([P, S], F32, name=f"yw{t}", tag=f"bank{PACK + t}") for t in rows]
        d0_win = [keep.tile([P, 3 * S], F32, name=f"d0_win{t}") for t in rows]
        wgt_win = [keep.tile([P, 3 * S], F32, name=f"wgt_win{t}") for t in rows]
        d1_win = [keep.tile([P, 2 * S], F32, name=f"d1_win{t}") for t in rows]
        d2_win = [keep.tile([P, 2 * S], F32, name=f"d2_win{t}") for t in rows]
        da = [keep.tile([P, S], F32, name=f"da{t}") for t in rows]
        cu = [keep.tile([P, S], F32, name=f"cu{t}") for t in rows]
        db = [keep.tile([P, S], F32, name=f"db{t}") for t in rows]
        gain = keep.tile([P, PACK, S], F32, name="gain")
        dd = keep.tile([P, PACK, S], F32, name="dd")
        hid = keep.tile([P, PACK, S], F32, name="hid")
        first, second, third = slice(0, S), slice(S, 2 * S), slice(2 * S, 3 * S)

        for h in range(2):
            for t in rows:
                cols = slice(h * HALF, (h + 1) * HALF)
                product(y[t][:, cols], w1, s1, t, xw[h][:], xs[h][:])
                nc.scalar.activation(wgt_win[t][:, S + h * HALF : S + (h + 1) * HALF], y[t][:, cols], ACT.Sigmoid, scale=-1.0)
        for t in rows:
            for h in range(2):
                product(yw[t][:, h * HALF : (h + 1) * HALF], w2, s2, t, xw[h][:], xs[h][:])
            nc.scalar.activation(wgt_win[t][:, third], yw[t][:], ACT.Sigmoid, scale=-1.0)

        def logarithms(t):
            if t == 0:
                nc.scalar.activation(d0_win[t][:, third], wgt_win[t][:, third], ACT.Ln, bias=tiny[:])
                nc.scalar.activation(d0_win[t][:, second], wgt_win[t][:, second], ACT.Ln, bias=tiny[:])
            else:
                nc.scalar.activation(d0_win[t][:, S:], wgt_win[t][:, S:], ACT.Ln, bias=tiny[:])

        def softplus(t):
            if t in FUSED:
                nc.vector.scalar_tensor_tensor(wgt_win[t][:, first], d0_win[t][:, third], -1.0, yw[t][:], ALU.mult, ALU.max)
                nc.vector.tensor_scalar(da[t][:], wgt_win[t][:, first], STEP, None, ALU.mult)
                nc.vector.scalar_tensor_tensor(d0_win[t][:, first], d0_win[t][:, second], -1.0, y[t][:], ALU.mult, ALU.max)
            else:
                nc.vector.scalar_tensor_tensor(d0_win[t][:, first], d0_win[t][:, second], -1.0, y[t][:], ALU.mult, ALU.max)
                nc.vector.scalar_tensor_tensor(wgt_win[t][:, first], d0_win[t][:, third], -1.0, yw[t][:], ALU.mult, ALU.max)

        def fetch_da(t):
            if t not in FUSED:
                nc.scalar.activation(da[t][:], d0_win[t][:].indirect(u1_sb[:]), ACT.Copy)

        def fetch_cu(t):
            nc.scalar.activation(cu[t][:], wgt_win[t][:].indirect(u1_sb[:]), ACT.Copy, scale=STEP)

        def offer_one(t):
            if t in FUSED:
                nc.vector.tensor_tensor(d1_win[t][:, second], d0_win[t][:].indirect(u1_sb[:]), da[t][:], ALU.add)
            else:
                nc.vector.scalar_tensor_tensor(d1_win[t][:, second], wgt_win[t][:, first], STEP, da[t][:], ALU.mult, ALU.add)

        def relax_one(t):
            nc.vector.tensor_tensor(d1_win[t][:, first], d0_win[t][:, first], d1_win[t][:, second], ALU.min)

        def fetch_db(t):
            if t not in FUSED_TWO:
                nc.scalar.activation(db[t][:], d1_win[t][:].indirect(u2_sb[:]), ACT.Copy)

        def offer_two(t):
            if t in FUSED_TWO:
                nc.vector.tensor_tensor(d2_win[t][:, second], d1_win[t][:].indirect(u2_sb[:]), cu[t][:], ALU.add)
            else:
                nc.vector.tensor_tensor(d2_win[t][:, second], db[t][:], cu[t][:], ALU.add)

        def relax_two(t):
            nc.vector.tensor_tensor(d2_win[t][:, first], d1_win[t][:, first], d2_win[t][:, second], ALU.min)

        def improvement(t, cols=first):
            nc.vector.tensor_tensor(da[t][:, cols], d0_win[t][:, cols], d2_win[t][:, cols], ALU.subtract)

        def weigh(t, cols=first):
            nc.vector.scalar_tensor_tensor(gain[:, t, cols], da[t][:, cols], unit_sb[:, t : t + 1], wgt_win[t][:, cols], ALU.mult, ALU.mult)

        def fetch_dd(t, cols=first):
            picks = u2_sb[:, cols.start // 16 : cols.stop // 16]
            nc.scalar.activation(dd[:, t, cols], d2_win[t][:].indirect(picks), ACT.Copy)

        def combine(t, cols=first):
            nc.vector.scalar_tensor_tensor(hid[:, t, cols], dd[:, t, cols], unit_sb[:, t : t + 1], gain[:, t, cols], ALU.mult, ALU.add)

        relax = [logarithms, softplus, fetch_da, offer_one, relax_one, fetch_cu, fetch_db, offer_two, relax_two]
        whole = relax + [fetch_dd, improvement, weigh, combine]
        for k in range(len(whole) + SKEW * (PACK - 1)):
            for t in rows:
                stages = whole if t < EARLY else relax
                if 0 <= k - SKEW * t < len(stages):
                    stages[k - SKEW * t](t)

        out_codes = keep.tile([P, S], U32, name="out_codes", align_bytes=64)
        out_scales = keep.tile([P, S], U8, name="out_scales", align_bytes=64)
        out_rows = out_0.rearrange("(p t) j -> p t j", t=PACK)
        out_words = out_1[0].rearrange("p n t -> p (n t)").bitcast(I32)

        def last_product(c):
            cols = slice(c * CHUNK, (c + 1) * CHUNK)
            if c * CHUNK % HALF == 0:
                for stage in whole[len(relax) :]:
                    for t in range(EARLY, PACK):
                        stage(t, slice(c * CHUNK, c * CHUNK + HALF))
            woven = keep.tile([P, CHUNK, PACK], BF16, name=f"woven{c}", align_bytes=64)
            weave = nc.scalar.copy if c < CHUNKS // 2 else nc.vector.tensor_copy
            weave(
                woven[:].rearrange("p (g i) t -> p g t i", i=4),
                hid[:, :, cols].rearrange("p t (g i) -> p g t i", i=4),
            )
            codes = keep.tile([P, CHUNK], U32, name=f"codes{c}", align_bytes=64)
            scales = keep.tile([P, CHUNK], U8, name=f"scales{c}", align_bytes=64)
            nc.vector.quantize_mx(codes[:].bitcast(FP8X4), scales[:], woven[:].rearrange("p j t -> p (j t)"))
            acc = psum.tile([P, PACK, CHUNK], F32, name=f"acc{c}", tag=f"bank{c}")
            for t in rows:
                product(acc[:, t, :], w3, s3, t, codes[:], scales[:])
            return acc

        def hand_out(c, acc):
            cols = slice(c * CHUNK, (c + 1) * CHUNK)
            rounded = keep.tile([P, CHUNK, PACK], BF16, name=f"rounded{c}", align_bytes=64)
            result = keep.tile([P, PACK, CHUNK], F32, name=f"result{c}")
            if c < CHUNKS - 1:
                nc.scalar.copy(result[:], acc[:])
                nc.scalar.copy(rounded[:], acc[:].rearrange("p t j -> p j t"))
            else:
                nc.vector.tensor_copy(result[:], acc[:])
                nc.vector.tensor_copy(
                    rounded[:].rearrange("p (g i) t -> p g t i", i=4),
                    result[:].rearrange("p t (g i) -> p g t i", i=4),
                )
            nc.sync.dma_start(out_rows[:, :, cols], result[:])
            nc.vector.quantize_mx(out_codes[:, cols].bitcast(FP8X4), out_scales[:, cols], rounded[:].rearrange("p j t -> p (j t)"))
            nc.sync.dma_start(out_words[:, cols], out_codes[:, cols].bitcast(I32))

        accs = [last_product(0)]
        for c in range(1, CHUNKS):
            accs.append(last_product(c))
            hand_out(c - 1, accs[c - 1])
        hand_out(CHUNKS - 1, accs[CHUNKS - 1])
        for q in range(4):
            queue = nc.scalar if q % 2 else nc.sync
            queue.dma_start(out_2[0, 4 * q : 4 * q + 4, :].bitcast(I32), out_scales[32 * q : 32 * q + 4, :].bitcast(I32))
